import numpy as np
import ml_dtypes


def mxq(x, axis, fmt="e4m3"):
    dtype, down = {"e4m3": (ml_dtypes.float8_e4m3fn, 7), "e5m2": (ml_dtypes.float8_e5m2, 14)}[fmt]
    v = np.moveaxis(np.asarray(x, np.float32).astype(ml_dtypes.bfloat16).astype(np.float64), axis, -1)
    blocks = v.reshape(v.shape[:-1] + (-1, 32))
    amax = np.abs(blocks).max(-1, keepdims=True)
    byte = np.maximum(np.where(amax > 0, np.frexp(amax)[1] - 1 + 127, 0) - down, 1)
    scale = np.exp2(byte - 127.0)
    codes = (blocks / scale).astype(np.float32).astype(dtype).astype(np.float64)
    return np.moveaxis((codes * scale).reshape(v.shape), -1, axis)


WIDE = False


def mx_kscale(k):
    if not WIDE:
        return np.ones(k)
    levels = np.array([10, -10, 5, -5, 0])
    if k % 512:
        return np.exp2(np.random.permutation(np.resize(levels, k // 32))).repeat(32)
    a = np.empty((k // 512, 16))
    for p in range(k // 512):
        a[p, :8] = np.random.permutation(np.resize(levels, 8))
        for g in range(8):
            far = levels[np.abs(levels - a[p, g]) >= 10]
            a[p, g + 8] = far[np.random.randint(len(far))]
    return np.exp2(a.ravel()).repeat(32)


def f64(x):
    return np.asarray(x).astype(np.float64)


def striped(idx):
    return np.tile(np.asarray(idx).reshape(-1, 16).T, (8, 1)).astype(np.uint16)


def unstriped(offs):
    return offs[:16].T.reshape(-1).astype(np.int64)


E2M1 = np.array([0.0, 0.5, 1.0, 1.5, 2.0, 3.0, 4.0, 6.0, -0.0, -0.5, -1.0, -1.5, -2.0, -3.0, -4.0, -6.0])


def pack_weight(w, fmt):
    k, n = w.shape
    w = f64(np.asarray(w, np.float32).astype(ml_dtypes.bfloat16)).reshape(k // 32, 32, n)
    amax = np.abs(w).max(1)
    if fmt == "e4m3":
        byte = np.frexp(amax)[1] - 1 + 127 - 7
    else:
        mant, ex = np.frexp(amax / 6.0)
        byte = np.where(mant > 0.5, ex, ex - 1) + 127
    byte = np.clip(np.where(amax > 0, byte, 1), 1, 254)
    scaled = (w * np.exp2(127.0 - byte)[:, None, :]).reshape(k, n).astype(np.float32)
    by_word = np.ascontiguousarray(scaled.reshape(k // 512, 128, 4, n).transpose(0, 1, 3, 2))
    if fmt == "e4m3":
        words = by_word.astype(ml_dtypes.float8_e4m3fn).view(np.uint8)
    else:
        c = by_word.astype(ml_dtypes.float4_e2m1fn).view(np.uint8) & 0xF
        words = (c[..., 0::2] | (c[..., 1::2] << 4)).reshape(k // 512, 128, 2 * n)
    return np.ascontiguousarray(words), np.ascontiguousarray(byte.astype(np.uint8).reshape(k // 512, 16, n))


def unpack_weight(words, scales, fmt):
    g, _, n = scales.shape
    words = np.ascontiguousarray(words).reshape(g, 128, n, -1)
    if fmt == "e4m3":
        vals = words.view(ml_dtypes.float8_e4m3fn).astype(np.float64)
    else:
        nib = np.empty((g, 128, n, 4), np.uint8)
        nib[..., 0::2] = words & 0xF
        nib[..., 1::2] = words >> 4
        vals = E2M1[nib]
    vals = vals * np.repeat(np.exp2(scales.astype(np.float64) - 127.0), 8, axis=1)[..., None]
    return vals.transpose(0, 1, 3, 2).reshape(g * 512, n)


D, T, I, Q, E, U, G = 512, 2048, 1024, 128, 512, 512, 64


def setup_inputs():
    n = np.random.standard_normal
    idx = np.random.permutation(T)[:I]
    idx2 = np.random.permutation(U)[:G]
    fd = mx_kscale(D)
    fi = mx_kscale(I)
    ti = np.ones(T)
    ti[idx] = fi
    keysp = pack_weight(n((D, T)) / fd[:, None], "e4m3")
    return {
        "query": (n((D, Q)) * 0.4 / np.sqrt(D) * fd[:, None]).astype(np.float32),
        "keys_words": keysp[0],
        "keys_scales": keysp[1],
        "prior": (0.5 * n((Q, U))).astype(np.float32),
        "trust": (np.random.uniform(0.4, 1.2, (Q, 1))).astype(np.float32),
        "size": (np.random.uniform(0.5, 2.0, (1, I)) * fi).astype(np.float32),
        "vals": (n((E, T)) / ti).astype(np.float32),
        "offs": striped(idx),
        "offs2": striped(idx2),
    }


def reference(query, keys_words, keys_scales, prior, trust, size, vals, offs, offs2):
    idx = unstriped(offs)
    idx2 = unstriped(offs2)
    keysu = unpack_weight(keys_words, keys_scales, "e4m3")
    queryq = mxq(f64(query), 0, "e4m3")
    keysidxg = keysu[:, idx]
    a = queryq.T @ keysidxg
    b = f64(prior)[:, idx2] * f64(trust) - a.reshape(Q, G, I // G).mean(axis=2)
    br = np.repeat(b, I // G, axis=1)
    s = a + br
    p = np.exp(s - np.max(s, axis=1, keepdims=True))
    w = p * f64(size) / np.sum(p, axis=1, keepdims=True)
    wt = w.T
    vt = f64(vals)[:, idx].T
    wtq = mxq(wt, 0, "e4m3")
    vtq = mxq(vt, 0, "e4m3")
    o = wtq.T @ vtq
    return o

@@ -1,0 +1,248 @@
+from contextlib import ExitStack
+
+import concourse.mybir as mybir
+from concourse.masks import make_identity
+
+D, T, I, Q, E, U, G = 512, 2048, 1024, 128, 512, 512, 64
+FLOPS = 2 * Q * I * D + 2 * Q * I * E
+
+F32 = mybir.dt.float32
+BF16 = mybir.dt.bfloat16
+I32 = mybir.dt.int32
+U32 = mybir.dt.uint32
+U16 = mybir.dt.uint16
+U8 = mybir.dt.uint8
+FP8X4 = mybir.dt.float8_e4m3fn_x4
+ALU = mybir.AluOpType
+ACT = mybir.ActivationFunctionType
+AX = mybir.AxisListType
+
+P = 128
+PACK = 4
+PASS = P * PACK
+PASSES = I // PASS
+PAGE = I // G
+LIST_COLS = PASS // 16
+
+
+def tile_attend_pagecentred_kernel(tc, query, keys_words, keys_scales, prior, trust, size, vals, offs, offs2, out):
+    nc = tc.nc
+    with ExitStack() as ctx:
+        keep = ctx.enter_context(tc.tile_pool(name="keep", bufs=1))
+        psum = ctx.enter_context(tc.psum_pool(name="psum", bufs=1))
+        turn = ctx.enter_context(tc.psum_pool(name="turn", bufs=4))
+
+        slots = keep.tile([P, I // 16], U16, name="slots")
+        nc.sync.dma_start(slots[:], offs)
+        key_scales = keep.tile([P, T], U8, name="key_scales", align_bytes=64)
+        nc.gpsimd.memset(key_scales[:].bitcast(I32), 0)
+        for quad in range(4):
+            nc.sync.dma_start(
+                key_scales[32 * quad : 32 * quad + 4, :].bitcast(I32),
+                keys_scales[0, 4 * quad : 4 * quad + 4, :].bitcast(I32),
+            )
+        pages = keep.tile([P, G // 16], U16, name="pages")
+        nc.sync.dma_start(pages[:], offs2)
+        key_words = keep.tile([P, T], I32, name="key_words", align_bytes=64)
+        nc.sync.dma_start(key_words[:], keys_words[0].rearrange("p n t -> p (n t)").bitcast(I32))
+
+        q_raw = keep.tile([P, PACK, Q], F32, name="q_raw")
+        nc.sync.dma_start(q_raw[:], query.rearrange("(p j) q -> p j q", j=PACK))
+
+        def load_pieces(f, cuts):
+            pieces = []
+            for lo, hi in zip(cuts[:-1], cuts[1:]):
+                piece = keep.tile([P, hi - lo], F32, name="vals_%d_%d" % (f, lo))
+                nc.sync.dma_start(piece[:], vals[f * P : (f + 1) * P, lo:hi])
+                pieces.append((lo, hi, piece))
+            return pieces
+
+        def load_whole(f):
+            whole = keep.tile([P, T], F32, name="vals_%d" % f, tag="vals_%d" % f, align_bytes=64)
+            nc.sync.dma_start(whole[:], vals[f * P : (f + 1) * P, :])
+            return whole
+
+        raw0 = load_pieces(0, (0, 1024, 1536, 2048))
+        prior_sb = keep.tile([P, U], F32, name="prior_sb")
+        nc.sync.dma_start(prior_sb[:], prior)
+        trust_sb = keep.tile([P, 1], F32, name="trust_sb")
+        nc.sync.dma_start(trust_sb[:], trust)
+        size_cols = keep.tile([P, PASSES, PACK], F32, name="size_cols")
+        nc.sync.dma_start(size_cols[:], size.rearrange("o (h p c) -> p (o h) c", h=PASSES, c=PACK))
+        raw1 = load_pieces(1, (0, 1024, 2048))
+        raw2 = load_whole(2)
+        raw3 = load_whole(3)
+
+        ident = keep.tile([P, P], F32, name="ident")
+        make_identity(nc, ident[:])
+        warm = keep.tile([P, 1], F32, name="warm")
+        nc.vector.memset(warm[:], 0.0)
+        nc.scalar.activation(warm[:], warm[:], ACT.Exp)
+
+        q_grouped = keep.tile([P, Q, PACK], BF16, name="q_grouped", tag="k_codes_1", align_bytes=64)
+        nc.scalar.copy(q_grouped[:], q_raw[:].rearrange("p j q -> p q j"))
+
+        k_scales = keep.tile([P, I], U8, name="k_scales", align_bytes=64)
+        nc.vector.tensor_copy(k_scales[:], key_scales[:].indirect(slots[:]))
+
+        def pass_list(h):
+            return slots[:, h * LIST_COLS : (h + 1) * LIST_COLS]
+
+        def gather_keys(h):
+            codes = keep.tile([P, PASS], U32, name="k_codes_%d" % h, tag="k_codes_%d" % h, align_bytes=64)
+            nc.vector.tensor_copy(codes[:], key_words[:].bitcast(U32).indirect(pass_list(h)))
+            return codes
+
+        k_codes = [gather_keys(0)]
+        q_codes = keep.tile([P, Q], U32, name="q_codes", align_bytes=64)
+        q_scales = keep.tile([P, Q], U8, name="q_scales", align_bytes=64)
+        nc.vector.quantize_mx(q_codes[:].bitcast(FP8X4), q_scales[:], q_grouped[:].rearrange("p q j -> p (q j)"))
+        k_codes.append(gather_keys(1))
+
+        scores = []
+        for h in range(PASSES):
+            bank = psum.tile([P, PASS], F32, name="scores_%d" % h, tag="bank_%d" % h)
+            nc.tensor.matmul_mx(
+                out=bank[:],
+                lhsT=q_codes[:].bitcast(FP8X4),
+                lhsT_scale=q_scales[:],
+                rhs=k_codes[h][:].bitcast(FP8X4),
+                rhs_scale=k_scales[:, h * PASS : (h + 1) * PASS],
+                start=True,
+                stop=True,
+            )
+            scores.append(bank)
+
+        pool0 = keep.tile([P, T], BF16, name="pool0")
+        for lo, hi, piece in raw0:
+            nc.scalar.activation(pool0[:, lo:hi], piece[:], ACT.Copy)
+
+        def gather_scalar(f, window):
+            picked = []
+            for h in range(PASSES):
+                g = keep.tile([P, PASS], BF16, name="picked_%d_%d" % (f, h))
+                nc.scalar.activation(g[:], window[:].indirect(pass_list(h)), ACT.Copy)
+                picked.append(g)
+            return picked
+
+        def gather_vector(f, window, h):
+            g = keep.tile([P, PASS], BF16, name="picked_%d_%d" % (f, h))
+            nc.vector.tensor_copy(g[:], window[:].indirect(pass_list(h)))
+            return g
+
+        def turn_pass(rows, grouped):
+            bank = turn.tile([P, 2, P], F32, name="turned")
+            words = rows.bitcast(F32)
+            for u in range(2):
+                nc.tensor.transpose(bank[:, u, :], words[:, u : PASS // 2 : 2], ident[:])
+            nc.scalar.copy(grouped.bitcast(F32).rearrange("p (r u) -> p r u", u=2), bank[:].rearrange("p u r -> p r u"))
+
+        def turn_both(name, rows):
+            grouped = keep.tile([P, I], BF16, name=name + "_grouped", align_bytes=64)
+            for h in range(PASSES):
+                turn_pass(rows[h], grouped[:, h * PASS : (h + 1) * PASS])
+            return grouped
+
+        picked0 = gather_scalar(0, pool0)
+
+        size_rows = []
+        for h in range(PASSES):
+            bank = psum.tile([P, PACK, P], F32, name="size_%d" % h, tag="bank_%d" % (PASSES + h))
+            for c in range(PACK):
+                nc.tensor.transpose(bank[:, c, :], size_cols[:, h, c : c + 1].to_broadcast([P, P]), ident[:])
+            size_rows.append(bank)
+
+        trust16 = keep.tile([P, 1], F32, name="trust16")
+        nc.gpsimd.tensor_scalar(trust16[:], trust_sb[:], float(PAGE), 0.0, ALU.mult, ALU.add)
+        prior_g = keep.tile([P, G], F32, name="prior_g")
+        nc.vector.tensor_copy(prior_g[:], prior_sb[:].indirect(pages[:]))
+        page_sums = keep.tile([P, G], F32, name="page_sums")
+        half_pages = G // PASSES
+        for h in range(PASSES):
+            nc.vector.tensor_reduce(
+                page_sums[:, h * half_pages : (h + 1) * half_pages],
+                scores[h][:].rearrange("p (g j) -> p g j", j=PAGE),
+                AX.X,
+                ALU.add,
+            )
+        shift16 = keep.tile([P, G], F32, name="shift16")
+        nc.vector.scalar_tensor_tensor(shift16[:], prior_g[:], trust16[:], page_sums[:], ALU.mult, ALU.subtract)
+        centred = keep.tile([P, I], F32, name="centred")
+        for h in range(PASSES):
+            nc.vector.scalar_tensor_tensor(
+                centred[:, h * PASS : (h + 1) * PASS].rearrange("p (g j) -> p g j", j=PAGE),
+                shift16[:, h * half_pages : (h + 1) * half_pages].unsqueeze(2).to_broadcast([P, half_pages, PAGE]),
+                1.0 / PAGE,
+                scores[h][:].rearrange("p (g j) -> p g j", j=PAGE),
+                ALU.mult,
+                ALU.add,
+            )
+        neg_max = keep.tile([P, 1], F32, name="neg_max")
+        nc.vector.tensor_reduce(neg_max[:], centred[:], AX.X, ALU.max, negate=True)
+
+        pool1 = keep.tile([P, T], BF16, name="pool1")
+        nc.scalar.activation(pool1[:, raw1[0][0] : raw1[0][1]], raw1[0][2][:], ACT.Copy)
+        nc.vector.tensor_copy(pool1[:, raw1[1][0] : raw1[1][1]], raw1[1][2][:])
+
+        probs = keep.tile([P, I], F32, name="probs")
+        row_sum = keep.tile([P, 1], F32, name="row_sum")
+        nc.scalar.activation(probs[:], centred[:], ACT.Exp, bias=neg_max[:], accum_out=row_sum[:])
+
+        grouped = {0: turn_both("v0", [g[:] for g in picked0])}
+        picked1 = gather_scalar(1, pool1)
+        picked2 = [gather_vector(2, raw2, h) for h in range(PASSES)]
+        inv_sum = keep.tile([P, 1], F32, name="inv_sum", tag="vals_2", align_bytes=64)
+        nc.vector.reciprocal(inv_sum[:], row_sum[:])
+        w_rows = []
+        for h in range(PASSES):
+            w = keep.tile([P, PASS], BF16, name="w_%d" % h)
+            nc.vector.scalar_tensor_tensor(
+                w[:].rearrange("q (p c) -> q p c", c=PACK),
+                probs[:, h * PASS : (h + 1) * PASS].rearrange("q (p c) -> q p c", c=PACK),
+                inv_sum[:],
+                size_rows[h][:].rearrange("q c p -> q p c"),
+                ALU.mult,
+                ALU.mult,
+            )
+            w_rows.append(w)
+        picked3 = [gather_vector(3, raw3, h) for h in range(PASSES)]
+        grouped[2] = turn_both("v2", [g[:] for g in picked2])
+        w_grouped = turn_both("w", [w[:] for w in w_rows])
+        grouped[1] = turn_both("v1", [g[:] for g in picked1])
+        grouped[3] = turn_both("v3", [g[:] for g in picked3])
+
+        width = PASSES * P
+        codes = keep.tile([P, 5 * width], U32, name="codes", tag="vals_3", align_bytes=64)
+        scales = keep.tile([P, 5 * width], U8, name="scales", align_bytes=64)
+
+        def quantize(place, rows, lo, hi):
+            cols = slice(place * width + lo * P, place * width + hi * P)
+            nc.vector.quantize_mx(codes[:, cols].bitcast(FP8X4), scales[:, cols], rows[:, lo * PASS : hi * PASS])
+
+        quantize(0, grouped[0], 0, PASSES)
+        quantize(4, w_grouped, 0, PASSES)
+        for f in (2, 1):
+            quantize(f, grouped[f], 0, PASSES)
+        for h in range(PASSES):
+            quantize(3, grouped[3], h, h + 1)
+
+        for f in (0, 2, 1, 3):
+            acc = psum.tile([P, P], F32, name="acc_%d" % f, tag="bank_%d" % f)
+            for h in range(PASSES):
+                w_cols = slice(4 * width + h * P, 4 * width + (h + 1) * P)
+                v_cols = slice(f * width + h * P, f * width + (h + 1) * P)
+                nc.tensor.matmul_mx(
+                    out=acc[:],
+                    lhsT=codes[:, w_cols].bitcast(FP8X4),
+                    lhsT_scale=scales[:, w_cols],
+                    rhs=codes[:, v_cols].bitcast(FP8X4),
+                    rhs_scale=scales[:, v_cols],
+                    start=(h == 0),
+                    stop=(h == PASSES - 1),
+                )
+            result = keep.tile([P, P], F32, name="result_%d" % f)
+            if f == 3:
+                nc.vector.tensor_copy(result[:], acc[:])
+            else:
+                nc.scalar.copy(result[:], acc[:])
+            nc.sync.dma_start(out[:, f * P : (f + 1) * P], result[:])

@@ -30,7 +30,7 @@ def tile_attend_pagecentred_kernel(tc, query, keys_words, keys_scales, prior, tr
     with ExitStack() as ctx:
         keep = ctx.enter_context(tc.tile_pool(name="keep", bufs=1))
         psum = ctx.enter_context(tc.psum_pool(name="psum", bufs=1))
-        turn = ctx.enter_context(tc.psum_pool(name="turn", bufs=4))
+        turn_pool = ctx.enter_context(tc.psum_pool(name="turn", bufs=4))
 
         slots = keep.tile([P, I // 16], U16, name="slots")
         nc.sync.dma_start(slots[:], offs)
@@ -52,7 +52,7 @@ def tile_attend_pagecentred_kernel(tc, query, keys_words, keys_scales, prior, tr
         def load_pieces(f, cuts):
             pieces = []
             for lo, hi in zip(cuts[:-1], cuts[1:]):
-                piece = keep.tile([P, hi - lo], F32, name="vals_%d_%d" % (f, lo))
+                piece = keep.tile([P, hi - lo], F32, name="vals_%d_%d" % (f, lo), tag="vals_%d_%d" % (f, lo))
                 nc.sync.dma_start(piece[:], vals[f * P : (f + 1) * P, lo:hi])
                 pieces.append((lo, hi, piece))
             return pieces
@@ -63,7 +63,7 @@ def tile_attend_pagecentred_kernel(tc, query, keys_words, keys_scales, prior, tr
             return whole
 
         raw0 = load_pieces(0, (0, 1024, 1536, 2048))
-        prior_sb = keep.tile([P, U], F32, name="prior_sb")
+        prior_sb = keep.tile([P, U], F32, name="prior_sb", tag="prior")
         nc.sync.dma_start(prior_sb[:], prior)
         trust_sb = keep.tile([P, 1], F32, name="trust_sb")
         nc.sync.dma_start(trust_sb[:], trust)
@@ -117,33 +117,24 @@ def tile_attend_pagecentred_kernel(tc, query, keys_words, keys_scales, prior, tr
         for lo, hi, piece in raw0:
             nc.scalar.activation(pool0[:, lo:hi], piece[:], ACT.Copy)
 
-        def gather_scalar(f, window):
-            picked = []
-            for h in range(PASSES):
-                g = keep.tile([P, PASS], BF16, name="picked_%d_%d" % (f, h))
-                nc.scalar.activation(g[:], window[:].indirect(pass_list(h)), ACT.Copy)
-                picked.append(g)
+        def gather_scalar(f, window, tag):
+            picked = keep.tile([P, I], BF16, name="picked_%d" % f, tag=tag)
+            nc.scalar.activation(picked[:], window[:].indirect(slots[:]), ACT.Copy)
             return picked
 
-        def gather_vector(f, window, h):
-            g = keep.tile([P, PASS], BF16, name="picked_%d_%d" % (f, h))
-            nc.vector.tensor_copy(g[:], window[:].indirect(pass_list(h)))
-            return g
-
-        def turn_pass(rows, grouped):
-            bank = turn.tile([P, 2, P], F32, name="turned")
+        def turn(rows, grouped, passes):
+            bank = turn_pool.tile([P, passes, 2, P], F32, name="turned")
             words = rows.bitcast(F32)
-            for u in range(2):
-                nc.tensor.transpose(bank[:, u, :], words[:, u : PASS // 2 : 2], ident[:])
-            nc.scalar.copy(grouped.bitcast(F32).rearrange("p (r u) -> p r u", u=2), bank[:].rearrange("p u r -> p r u"))
+            for h in range(passes):
+                for u in range(2):
+                    lo = h * PASS // 2
+                    nc.tensor.transpose(bank[:, h, u, :], words[:, lo + u : lo + PASS // 2 : 2], ident[:])
+            nc.scalar.copy(
+                grouped.bitcast(F32).rearrange("p (h r u) -> p h r u", h=passes, u=2),
+                bank[:].rearrange("p h u r -> p h r u"),
+            )
 
-        def turn_both(name, rows):
-            grouped = keep.tile([P, I], BF16, name=name + "_grouped", align_bytes=64)
-            for h in range(PASSES):
-                turn_pass(rows[h], grouped[:, h * PASS : (h + 1) * PASS])
-            return grouped
-
-        picked0 = gather_scalar(0, pool0)
+        picked0 = gather_scalar(0, pool0, "picked_0")
 
         size_rows = []
         for h in range(PASSES):
@@ -154,83 +145,93 @@ def tile_attend_pagecentred_kernel(tc, query, keys_words, keys_scales, prior, tr
 
         trust16 = keep.tile([P, 1], F32, name="trust16")
         nc.gpsimd.tensor_scalar(trust16[:], trust_sb[:], float(PAGE), 0.0, ALU.mult, ALU.add)
+        half_pages = G // PASSES
+
+        def sum_pages(h, tag):
+            sums = keep.tile([P, half_pages], F32, name="page_sums_%d" % h, tag=tag)
+            nc.vector.tensor_reduce(sums[:], scores[h][:].rearrange("p (g j) -> p g j", j=PAGE), AX.X, ALU.add)
+            return sums
+
+        page_sums = [sum_pages(0, "page_sums_0")]
         prior_g = keep.tile([P, G], F32, name="prior_g")
         nc.vector.tensor_copy(prior_g[:], prior_sb[:].indirect(pages[:]))
-        page_sums = keep.tile([P, G], F32, name="page_sums")
-        half_pages = G // PASSES
+        page_sums.append(sum_pages(1, "prior"))
+        shift16 = []
         for h in range(PASSES):
-            nc.vector.tensor_reduce(
-                page_sums[:, h * half_pages : (h + 1) * half_pages],
-                scores[h][:].rearrange("p (g j) -> p g j", j=PAGE),
-                AX.X,
-                ALU.add,
+            shift = keep.tile([P, half_pages], F32, name="shift16_%d" % h)
+            nc.vector.scalar_tensor_tensor(
+                shift[:], prior_g[:, h * half_pages : (h + 1) * half_pages], trust16[:], page_sums[h][:], ALU.mult, ALU.subtract
             )
-        shift16 = keep.tile([P, G], F32, name="shift16")
-        nc.vector.scalar_tensor_tensor(shift16[:], prior_g[:], trust16[:], page_sums[:], ALU.mult, ALU.subtract)
-        centred = keep.tile([P, I], F32, name="centred")
+            shift16.append(shift)
+        centred = keep.tile([P, I], F32, name="centred", tag="centred")
         for h in range(PASSES):
             nc.vector.scalar_tensor_tensor(
                 centred[:, h * PASS : (h + 1) * PASS].rearrange("p (g j) -> p g j", j=PAGE),
-                shift16[:, h * half_pages : (h + 1) * half_pages].unsqueeze(2).to_broadcast([P, half_pages, PAGE]),
+                shift16[h][:].unsqueeze(2).to_broadcast([P, half_pages, PAGE]),
                 1.0 / PAGE,
                 scores[h][:].rearrange("p (g j) -> p g j", j=PAGE),
                 ALU.mult,
                 ALU.add,
             )
-        neg_max = keep.tile([P, 1], F32, name="neg_max")
-        nc.vector.tensor_reduce(neg_max[:], centred[:], AX.X, ALU.max, negate=True)
 
         pool1 = keep.tile([P, T], BF16, name="pool1")
-        nc.scalar.activation(pool1[:, raw1[0][0] : raw1[0][1]], raw1[0][2][:], ACT.Copy)
-        nc.vector.tensor_copy(pool1[:, raw1[1][0] : raw1[1][1]], raw1[1][2][:])
+        for lo, hi, piece in raw1:
+            nc.scalar.activation(pool1[:, lo:hi], piece[:], ACT.Copy)
+        neg_max = keep.tile([P, 1], F32, name="neg_max")
+        nc.vector.tensor_reduce(neg_max[:], centred[:], AX.X, ALU.max, negate=True)
 
         probs = keep.tile([P, I], F32, name="probs")
         row_sum = keep.tile([P, 1], F32, name="row_sum")
         nc.scalar.activation(probs[:], centred[:], ACT.Exp, bias=neg_max[:], accum_out=row_sum[:])
 
-        grouped = {0: turn_both("v0", [g[:] for g in picked0])}
-        picked1 = gather_scalar(1, pool1)
-        picked2 = [gather_vector(2, raw2, h) for h in range(PASSES)]
+        early = keep.tile([P, 2 * I], BF16, name="early", align_bytes=64)
+        late = keep.tile([P, 2 * I], BF16, name="late", align_bytes=64)
+        last = keep.tile([P, I], BF16, name="last", align_bytes=64)
+        turn(picked0[:], early[:, I : 2 * I], PASSES)
+        picked1 = gather_scalar(1, pool1, "centred")
+        picked2 = keep.tile([P, I], BF16, name="picked_2")
+        nc.vector.tensor_copy(picked2[:], raw2[:].indirect(slots[:]))
         inv_sum = keep.tile([P, 1], F32, name="inv_sum", tag="vals_2", align_bytes=64)
         nc.vector.reciprocal(inv_sum[:], row_sum[:])
-        w_rows = []
+        w_rows = keep.tile([P, I], BF16, name="w_rows")
         for h in range(PASSES):
-            w = keep.tile([P, PASS], BF16, name="w_%d" % h)
             nc.vector.scalar_tensor_tensor(
-                w[:].rearrange("q (p c) -> q p c", c=PACK),
+                w_rows[:, h * PASS : (h + 1) * PASS].rearrange("q (p c) -> q p c", c=PACK),
                 probs[:, h * PASS : (h + 1) * PASS].rearrange("q (p c) -> q p c", c=PACK),
                 inv_sum[:],
                 size_rows[h][:].rearrange("q c p -> q p c"),
                 ALU.mult,
                 ALU.mult,
             )
-            w_rows.append(w)
-        picked3 = [gather_vector(3, raw3, h) for h in range(PASSES)]
-        grouped[2] = turn_both("v2", [g[:] for g in picked2])
-        w_grouped = turn_both("w", [w[:] for w in w_rows])
-        grouped[1] = turn_both("v1", [g[:] for g in picked1])
-        grouped[3] = turn_both("v3", [g[:] for g in picked3])
+        picked3 = []
+        for h in range(PASSES):
+            picked = keep.tile([P, PASS], BF16, name="picked_3_%d" % h)
+            nc.vector.tensor_copy(picked[:], raw3[:].indirect(pass_list(h)))
+            picked3.append(picked)
+        turn(w_rows[:], early[:, 0:I], PASSES)
+        turn(picked2[:], late[:, 0:I], PASSES)
+        turn(picked1[:], late[:, I : 2 * I], PASSES)
+        for h in range(PASSES):
+            turn(picked3[h][:], last[:, h * PASS : (h + 1) * PASS], 1)
 
         width = PASSES * P
         codes = keep.tile([P, 5 * width], U32, name="codes", tag="vals_3", align_bytes=64)
         scales = keep.tile([P, 5 * width], U8, name="scales", align_bytes=64)
 
-        def quantize(place, rows, lo, hi):
-            cols = slice(place * width + lo * P, place * width + hi * P)
-            nc.vector.quantize_mx(codes[:, cols].bitcast(FP8X4), scales[:, cols], rows[:, lo * PASS : hi * PASS])
+        def quantize(first, rows):
+            cols = slice(first, first + rows.shape[1] // PACK)
+            nc.vector.quantize_mx(codes[:, cols].bitcast(FP8X4), scales[:, cols], rows)
 
-        quantize(0, grouped[0], 0, PASSES)
-        quantize(4, w_grouped, 0, PASSES)
-        for f in (2, 1):
-            quantize(f, grouped[f], 0, PASSES)
+        quantize(0, early[:])
+        quantize(2 * width, late[:])
         for h in range(PASSES):
-            quantize(3, grouped[3], h, h + 1)
+            quantize(4 * width + h * P, last[:, h * PASS : (h + 1) * PASS])
 
-        for f in (0, 2, 1, 3):
+        for place, f in enumerate((0, 2, 1, 3)):
             acc = psum.tile([P, P], F32, name="acc_%d" % f, tag="bank_%d" % f)
             for h in range(PASSES):
-                w_cols = slice(4 * width + h * P, 4 * width + (h + 1) * P)
-                v_cols = slice(f * width + h * P, f * width + (h + 1) * P)
+                w_cols = slice(h * P, (h + 1) * P)
+                v_cols = slice((place + 1) * width + h * P, (place + 1) * width + (h + 1) * P)
                 nc.tensor.matmul_mx(
                     out=acc[:],
                     lhsT=codes[:, w_cols].bitcast(FP8X4),

@@ -35,7 +35,7 @@ def tile_attend_pagecentred_kernel(tc, query, keys_words, keys_scales, prior, tr
         slots = keep.tile([P, I // 16], U16, name="slots")
         nc.sync.dma_start(slots[:], offs)
         key_scales = keep.tile([P, T], U8, name="key_scales", align_bytes=64)
-        nc.gpsimd.memset(key_scales[:].bitcast(I32), 0)
+        nc.vector.memset(key_scales[:].bitcast(I32), 0)
         for quad in range(4):
             nc.sync.dma_start(
                 key_scales[32 * quad : 32 * quad + 4, :].bitcast(I32),
@@ -45,8 +45,7 @@ def tile_attend_pagecentred_kernel(tc, query, keys_words, keys_scales, prior, tr
         nc.sync.dma_start(pages[:], offs2)
         key_words = keep.tile([P, T], I32, name="key_words", align_bytes=64)
         nc.sync.dma_start(key_words[:], keys_words[0].rearrange("p n t -> p (n t)").bitcast(I32))
-
-        q_raw = keep.tile([P, PACK, Q], F32, name="q_raw")
+        q_raw = keep.tile([P, PACK, Q], F32, name="q_raw", tag="k_codes_1", align_bytes=64)
         nc.sync.dma_start(q_raw[:], query.rearrange("(p j) q -> p j q", j=PACK))
 
         def load_pieces(f, cuts):
@@ -63,30 +62,32 @@ def tile_attend_pagecentred_kernel(tc, query, keys_words, keys_scales, prior, tr
             return whole
 
         raw0 = load_pieces(0, (0, 1024, 1536, 2048))
-        prior_sb = keep.tile([P, U], F32, name="prior_sb", tag="prior")
+        prior_sb = keep.tile([P, U], F32, name="prior_sb")
         nc.sync.dma_start(prior_sb[:], prior)
-        trust_sb = keep.tile([P, 1], F32, name="trust_sb")
+        trust_sb = keep.tile([P, 1], F32, name="trust_sb", tag="trust")
         nc.sync.dma_start(trust_sb[:], trust)
         size_cols = keep.tile([P, PASSES, PACK], F32, name="size_cols")
         nc.sync.dma_start(size_cols[:], size.rearrange("o (h p c) -> p (o h) c", h=PASSES, c=PACK))
-        raw1 = load_pieces(1, (0, 1024, 2048))
+        raw1 = load_pieces(1, (0, 512, 2048))
         raw2 = load_whole(2)
         raw3 = load_whole(3)
 
+        warm = keep.tile([P, 1], F32, name="warm")
+        nc.gpsimd.memset(warm[:], 0.0)
+        nc.scalar.activation(warm[:], warm[:], ACT.Exp)
         ident = keep.tile([P, P], F32, name="ident")
         make_identity(nc, ident[:])
-        warm = keep.tile([P, 1], F32, name="warm")
-        nc.vector.memset(warm[:], 0.0)
-        nc.scalar.activation(warm[:], warm[:], ACT.Exp)
+        minus_one = keep.tile([P, 1], F32, name="minus_one")
+        nc.gpsimd.memset(minus_one[:], -1.0)
 
-        q_grouped = keep.tile([P, Q, PACK], BF16, name="q_grouped", tag="k_codes_1", align_bytes=64)
+        q_grouped = keep.tile([P, Q, PACK], BF16, name="q_grouped", align_bytes=64)
         nc.scalar.copy(q_grouped[:], q_raw[:].rearrange("p j q -> p q j"))
-
-        k_scales = keep.tile([P, I], U8, name="k_scales", align_bytes=64)
-        nc.vector.tensor_copy(k_scales[:], key_scales[:].indirect(slots[:]))
 
         def pass_list(h):
             return slots[:, h * LIST_COLS : (h + 1) * LIST_COLS]
+
+        k_scales = keep.tile([P, I], U8, name="k_scales", align_bytes=64)
+        nc.vector.tensor_copy(k_scales[:], key_scales[:].indirect(slots[:]))
 
         def gather_keys(h):
             codes = keep.tile([P, PASS], U32, name="k_codes_%d" % h, tag="k_codes_%d" % h, align_bytes=64)
@@ -122,14 +123,14 @@ def tile_attend_pagecentred_kernel(tc, query, keys_words, keys_scales, prior, tr
             nc.scalar.activation(picked[:], window[:].indirect(slots[:]), ACT.Copy)
             return picked
 
-        def turn(rows, grouped, passes):
-            bank = turn_pool.tile([P, passes, 2, P], F32, name="turned")
+        def turn(rows, grouped, passes, copy):
+            bank = turn_pool.tile([P, passes, 2, P], F32, name="turned", tag="turned")
             words = rows.bitcast(F32)
             for h in range(passes):
                 for u in range(2):
                     lo = h * PASS // 2
                     nc.tensor.transpose(bank[:, h, u, :], words[:, lo + u : lo + PASS // 2 : 2], ident[:])
-            nc.scalar.copy(
+            copy(
                 grouped.bitcast(F32).rearrange("p (h r u) -> p h r u", h=passes, u=2),
                 bank[:].rearrange("p h u r -> p h r u"),
             )
@@ -155,10 +156,10 @@ def tile_attend_pagecentred_kernel(tc, query, keys_words, keys_scales, prior, tr
         page_sums = [sum_pages(0, "page_sums_0")]
         prior_g = keep.tile([P, G], F32, name="prior_g")
         nc.vector.tensor_copy(prior_g[:], prior_sb[:].indirect(pages[:]))
-        page_sums.append(sum_pages(1, "prior"))
+        page_sums.append(sum_pages(1, "trust"))
         shift16 = []
         for h in range(PASSES):
-            shift = keep.tile([P, half_pages], F32, name="shift16_%d" % h)
+            shift = keep.tile([P, half_pages], F32, name="shift16_%d" % h, tag="shift16_%d" % h)
             nc.vector.scalar_tensor_tensor(
                 shift[:], prior_g[:, h * half_pages : (h + 1) * half_pages], trust16[:], page_sums[h][:], ALU.mult, ALU.subtract
             )
@@ -173,27 +174,27 @@ def tile_attend_pagecentred_kernel(tc, query, keys_words, keys_scales, prior, tr
                 ALU.mult,
                 ALU.add,
             )
-
-        pool1 = keep.tile([P, T], BF16, name="pool1")
-        for lo, hi, piece in raw1:
-            nc.scalar.activation(pool1[:, lo:hi], piece[:], ACT.Copy)
-        neg_max = keep.tile([P, 1], F32, name="neg_max")
-        nc.vector.tensor_reduce(neg_max[:], centred[:], AX.X, ALU.max, negate=True)
+        half_max = []
+        for h in range(PASSES):
+            part = keep.tile([P, 1], F32, name="half_max_%d" % h)
+            nc.vector.tensor_reduce(part[:], centred[:, h * PASS : (h + 1) * PASS], AX.X, ALU.max, negate=True)
+            half_max.append(part)
+        neg_max = keep.tile([P, 1], F32, name="neg_max", tag="neg_max", align_bytes=64)
+        nc.gpsimd.tensor_scalar(neg_max[:], half_max[0][:], half_max[1][:], None, ALU.min)
+        pool1 = keep.tile([P, T], BF16, name="pool1", tag="shift16_1")
+        nc.scalar.activation(pool1[:, raw1[0][0] : raw1[0][1]], raw1[0][2][:], ACT.Copy)
+        nc.vector.tensor_copy(pool1[:, raw1[1][0] : raw1[1][1]], raw1[1][2][:])
 
         probs = keep.tile([P, I], F32, name="probs")
-        row_sum = keep.tile([P, 1], F32, name="row_sum")
+        row_sum = keep.tile([P, 1], F32, name="row_sum", tag="inv_sum_dep")
         nc.scalar.activation(probs[:], centred[:], ACT.Exp, bias=neg_max[:], accum_out=row_sum[:])
-
-        early = keep.tile([P, 2 * I], BF16, name="early", align_bytes=64)
-        late = keep.tile([P, 2 * I], BF16, name="late", align_bytes=64)
-        last = keep.tile([P, I], BF16, name="last", align_bytes=64)
-        turn(picked0[:], early[:, I : 2 * I], PASSES)
+        inv_sum = keep.tile([P, 1], F32, name="inv_sum")
+        nc.gpsimd.tensor_tensor(inv_sum[:], row_sum[:], minus_one[:], ALU.pow)
         picked1 = gather_scalar(1, pool1, "centred")
-        picked2 = keep.tile([P, I], BF16, name="picked_2")
+        picked2 = keep.tile([P, I], BF16, name="picked_2", tag="picked_2")
         nc.vector.tensor_copy(picked2[:], raw2[:].indirect(slots[:]))
-        inv_sum = keep.tile([P, 1], F32, name="inv_sum", tag="vals_2", align_bytes=64)
-        nc.vector.reciprocal(inv_sum[:], row_sum[:])
-        w_rows = keep.tile([P, I], BF16, name="w_rows")
+
+        w_rows = keep.tile([P, I], BF16, name="w_rows", tag="vals_2", align_bytes=64)
         for h in range(PASSES):
             nc.vector.scalar_tensor_tensor(
                 w_rows[:, h * PASS : (h + 1) * PASS].rearrange("q (p c) -> q p c", c=PACK),
@@ -203,35 +204,39 @@ def tile_attend_pagecentred_kernel(tc, query, keys_words, keys_scales, prior, tr
                 ALU.mult,
                 ALU.mult,
             )
+
         picked3 = []
         for h in range(PASSES):
             picked = keep.tile([P, PASS], BF16, name="picked_3_%d" % h)
             nc.vector.tensor_copy(picked[:], raw3[:].indirect(pass_list(h)))
             picked3.append(picked)
-        turn(w_rows[:], early[:, 0:I], PASSES)
-        turn(picked2[:], late[:, 0:I], PASSES)
-        turn(picked1[:], late[:, I : 2 * I], PASSES)
+
+        grouped = keep.tile([P, 5 * I], BF16, name="grouped", tag="neg_max", align_bytes=64)
+        turn(picked0[:], grouped[:, I : 2 * I], PASSES, nc.scalar.copy)
+        turn(w_rows[:], grouped[:, 0:I], PASSES, nc.scalar.copy)
+        turn(picked1[:], grouped[:, 2 * I : 3 * I], PASSES, nc.scalar.copy)
+        turn(picked2[:], grouped[:, 3 * I : 4 * I], PASSES, nc.scalar.copy)
         for h in range(PASSES):
-            turn(picked3[h][:], last[:, h * PASS : (h + 1) * PASS], 1)
+            turn(picked3[h][:], grouped[:, 4 * I + h * PASS : 4 * I + (h + 1) * PASS], 1, nc.scalar.copy)
 
         width = PASSES * P
         codes = keep.tile([P, 5 * width], U32, name="codes", tag="vals_3", align_bytes=64)
         scales = keep.tile([P, 5 * width], U8, name="scales", align_bytes=64)
 
-        def quantize(first, rows):
-            cols = slice(first, first + rows.shape[1] // PACK)
-            nc.vector.quantize_mx(codes[:, cols].bitcast(FP8X4), scales[:, cols], rows)
+        def quantize(first, count):
+            cols = slice(first, first + count)
+            nc.vector.quantize_mx(codes[:, cols].bitcast(FP8X4), scales[:, cols], grouped[:, first * PACK : (first + count) * PACK])
 
-        quantize(0, early[:])
-        quantize(2 * width, late[:])
+        quantize(0, 2 * width)
+        quantize(2 * width, 2 * width)
         for h in range(PASSES):
-            quantize(4 * width + h * P, last[:, h * PASS : (h + 1) * PASS])
+            quantize(4 * width + h * P, P)
 
-        for place, f in enumerate((0, 2, 1, 3)):
+        for f in range(4):
             acc = psum.tile([P, P], F32, name="acc_%d" % f, tag="bank_%d" % f)
             for h in range(PASSES):
                 w_cols = slice(h * P, (h + 1) * P)
-                v_cols = slice((place + 1) * width + h * P, (place + 1) * width + (h + 1) * P)
+                v_cols = slice((f + 1) * width + h * P, (f + 1) * width + (h + 1) * P)
                 nc.tensor.matmul_mx(
                     out=acc[:],
                     lhsT=codes[:, w_cols].bitcast(FP8X4),

@@ -68,8 +68,9 @@ def tile_attend_pagecentred_kernel(tc, query, keys_words, keys_scales, prior, tr
         nc.sync.dma_start(trust_sb[:], trust)
         size_cols = keep.tile([P, PASSES, PACK], F32, name="size_cols")
         nc.sync.dma_start(size_cols[:], size.rearrange("o (h p c) -> p (o h) c", h=PASSES, c=PACK))
-        raw1 = load_pieces(1, (0, 512, 2048))
+        raw1 = load_pieces(1, (512, 2048))
         raw2 = load_whole(2)
+        raw1 = load_pieces(1, (0, 512)) + raw1
         raw3 = load_whole(3)
 
         warm = keep.tile([P, 1], F32, name="warm")
@@ -135,7 +136,11 @@ def tile_attend_pagecentred_kernel(tc, query, keys_words, keys_scales, prior, tr
                 bank[:].rearrange("p h u r -> p h r u"),
             )
 
-        picked0 = gather_scalar(0, pool0, "picked_0")
+        first = keep.tile([P, I], BF16, name="first", align_bytes=64)
+        for h in range(PASSES):
+            picked = keep.tile([P, PASS], BF16, name="picked_0_%d" % h)
+            nc.scalar.activation(picked[:], pool0[:].indirect(pass_list(h)), ACT.Copy)
+            turn(picked[:], first[:, h * PASS : (h + 1) * PASS], 1, nc.scalar.copy)
 
         size_rows = []
         for h in range(PASSES):
@@ -159,7 +164,7 @@ def tile_attend_pagecentred_kernel(tc, query, keys_words, keys_scales, prior, tr
         page_sums.append(sum_pages(1, "trust"))
         shift16 = []
         for h in range(PASSES):
-            shift = keep.tile([P, half_pages], F32, name="shift16_%d" % h, tag="shift16_%d" % h)
+            shift = keep.tile([P, half_pages], F32, name="shift16_%d" % h, tag="shift16_%d" % h, align_bytes=64)
             nc.vector.scalar_tensor_tensor(
                 shift[:], prior_g[:, h * half_pages : (h + 1) * half_pages], trust16[:], page_sums[h][:], ALU.mult, ALU.subtract
             )
@@ -181,8 +186,7 @@ def tile_attend_pagecentred_kernel(tc, query, keys_words, keys_scales, prior, tr
             half_max.append(part)
         neg_max = keep.tile([P, 1], F32, name="neg_max", tag="neg_max", align_bytes=64)
         nc.gpsimd.tensor_scalar(neg_max[:], half_max[0][:], half_max[1][:], None, ALU.min)
-        pool1 = keep.tile([P, T], BF16, name="pool1", tag="shift16_1")
-        nc.scalar.activation(pool1[:, raw1[0][0] : raw1[0][1]], raw1[0][2][:], ACT.Copy)
+        pool1 = keep.tile([P, T], BF16, name="pool1", tag="shift16_1", align_bytes=64)
         nc.vector.tensor_copy(pool1[:, raw1[1][0] : raw1[1][1]], raw1[1][2][:])
 
         probs = keep.tile([P, I], F32, name="probs")
@@ -190,11 +194,12 @@ def tile_attend_pagecentred_kernel(tc, query, keys_words, keys_scales, prior, tr
         nc.scalar.activation(probs[:], centred[:], ACT.Exp, bias=neg_max[:], accum_out=row_sum[:])
         inv_sum = keep.tile([P, 1], F32, name="inv_sum")
         nc.gpsimd.tensor_tensor(inv_sum[:], row_sum[:], minus_one[:], ALU.pow)
-        picked1 = gather_scalar(1, pool1, "centred")
+        nc.scalar.activation(pool1[:, raw1[0][0] : raw1[0][1]], raw1[0][2][:], ACT.Copy)
+        picked1 = gather_scalar(1, pool1, "picked_1")
         picked2 = keep.tile([P, I], BF16, name="picked_2", tag="picked_2")
         nc.vector.tensor_copy(picked2[:], raw2[:].indirect(slots[:]))
 
-        w_rows = keep.tile([P, I], BF16, name="w_rows", tag="vals_2", align_bytes=64)
+        w_rows = keep.tile([P, I], BF16, name="w_rows")
         for h in range(PASSES):
             nc.vector.scalar_tensor_tensor(
                 w_rows[:, h * PASS : (h + 1) * PASS].rearrange("q (p c) -> q p c", c=PACK),
@@ -211,32 +216,32 @@ def tile_attend_pagecentred_kernel(tc, query, keys_words, keys_scales, prior, tr
             nc.vector.tensor_copy(picked[:], raw3[:].indirect(pass_list(h)))
             picked3.append(picked)
 
-        grouped = keep.tile([P, 5 * I], BF16, name="grouped", tag="neg_max", align_bytes=64)
-        turn(picked0[:], grouped[:, I : 2 * I], PASSES, nc.scalar.copy)
+        grouped = keep.tile([P, 4 * I], BF16, name="grouped", tag="shift16_1", align_bytes=64)
+        turn(picked2[:], grouped[:, I : 2 * I], PASSES, nc.scalar.copy)
         turn(w_rows[:], grouped[:, 0:I], PASSES, nc.scalar.copy)
         turn(picked1[:], grouped[:, 2 * I : 3 * I], PASSES, nc.scalar.copy)
-        turn(picked2[:], grouped[:, 3 * I : 4 * I], PASSES, nc.scalar.copy)
         for h in range(PASSES):
-            turn(picked3[h][:], grouped[:, 4 * I + h * PASS : 4 * I + (h + 1) * PASS], 1, nc.scalar.copy)
+            turn(picked3[h][:], grouped[:, 3 * I + h * PASS : 3 * I + (h + 1) * PASS], 1, nc.scalar.copy)
 
         width = PASSES * P
         codes = keep.tile([P, 5 * width], U32, name="codes", tag="vals_3", align_bytes=64)
         scales = keep.tile([P, 5 * width], U8, name="scales", align_bytes=64)
 
-        def quantize(first, count):
-            cols = slice(first, first + count)
-            nc.vector.quantize_mx(codes[:, cols].bitcast(FP8X4), scales[:, cols], grouped[:, first * PACK : (first + count) * PACK])
+        def quantize(place, rows):
+            cols = slice(place, place + rows.shape[1] // PACK)
+            nc.vector.quantize_mx(codes[:, cols].bitcast(FP8X4), scales[:, cols], rows)
 
-        quantize(0, 2 * width)
-        quantize(2 * width, 2 * width)
+        quantize(4 * width, first[:])
+        quantize(0, grouped[:, 0 : 2 * I])
+        quantize(2 * width, grouped[:, 2 * I : 3 * I])
         for h in range(PASSES):
-            quantize(4 * width + h * P, P)
+            quantize(3 * width + h * P, grouped[:, 3 * I + h * PASS : 3 * I + (h + 1) * PASS])
 
-        for f in range(4):
+        for f, place in ((0, 4), (2, 1), (1, 2), (3, 3)):
             acc = psum.tile([P, P], F32, name="acc_%d" % f, tag="bank_%d" % f)
             for h in range(PASSES):
                 w_cols = slice(h * P, (h + 1) * P)
-                v_cols = slice((f + 1) * width + h * P, (f + 1) * width + (h + 1) * P)
+                v_cols = slice(place * width + h * P, place * width + (h + 1) * P)
                 nc.tensor.matmul_mx(
                     out=acc[:],
                     lhsT=codes[:, w_cols].bitcast(FP8X4),

@@ -73,9 +73,6 @@ def tile_attend_pagecentred_kernel(tc, query, keys_words, keys_scales, prior, tr
         raw1 = load_pieces(1, (0, 512)) + raw1
         raw3 = load_whole(3)
 
-        warm = keep.tile([P, 1], F32, name="warm")
-        nc.gpsimd.memset(warm[:], 0.0)
-        nc.scalar.activation(warm[:], warm[:], ACT.Exp)
         ident = keep.tile([P, P], F32, name="ident")
         make_identity(nc, ident[:])
         minus_one = keep.tile([P, 1], F32, name="minus_one")

from contextlib import ExitStack

import concourse.mybir as mybir
from concourse.masks import make_identity

D, T, I, Q, E, U, G = 512, 2048, 1024, 128, 512, 512, 64
FLOPS = 2 * Q * I * D + 2 * Q * I * E

F32 = mybir.dt.float32
BF16 = mybir.dt.bfloat16
I32 = mybir.dt.int32
U32 = mybir.dt.uint32
U16 = mybir.dt.uint16
U8 = mybir.dt.uint8
FP8X4 = mybir.dt.float8_e4m3fn_x4
ALU = mybir.AluOpType
ACT = mybir.ActivationFunctionType
AX = mybir.AxisListType

P = 128
PACK = 4
PASS = P * PACK
PASSES = I // PASS
PAGE = I // G
LIST_COLS = PASS // 16


def tile_attend_pagecentred_kernel(tc, query, keys_words, keys_scales, prior, trust, size, vals, offs, offs2, out):
    nc = tc.nc
    with ExitStack() as ctx:
        keep = ctx.enter_context(tc.tile_pool(name="keep", bufs=1))
        psum = ctx.enter_context(tc.psum_pool(name="psum", bufs=1))
        turn_pool = ctx.enter_context(tc.psum_pool(name="turn", bufs=4))

        slots = keep.tile([P, I // 16], U16, name="slots")
        nc.sync.dma_start(slots[:], offs)
        key_scales = keep.tile([P, T], U8, name="key_scales", align_bytes=64)
        nc.vector.memset(key_scales[:].bitcast(I32), 0)
        for quad in range(4):
            nc.sync.dma_start(
                key_scales[32 * quad : 32 * quad + 4, :].bitcast(I32),
                keys_scales[0, 4 * quad : 4 * quad + 4, :].bitcast(I32),
            )
        pages = keep.tile([P, G // 16], U16, name="pages")
        nc.sync.dma_start(pages[:], offs2)
        key_words = keep.tile([P, T], I32, name="key_words", align_bytes=64)
        nc.sync.dma_start(key_words[:], keys_words[0].rearrange("p n t -> p (n t)").bitcast(I32))
        q_raw = keep.tile([P, PACK, Q], F32, name="q_raw", tag="k_codes_1", align_bytes=64)
        nc.sync.dma_start(q_raw[:], query.rearrange("(p j) q -> p j q", j=PACK))

        def load_pieces(f, cuts):
            pieces = []
            for lo, hi in zip(cuts[:-1], cuts[1:]):
                piece = keep.tile([P, hi - lo], F32, name="vals_%d_%d" % (f, lo), tag="vals_%d_%d" % (f, lo))
                nc.sync.dma_start(piece[:], vals[f * P : (f + 1) * P, lo:hi])
                pieces.append((lo, hi, piece))
            return pieces

        def load_whole(f):
            whole = keep.tile([P, T], F32, name="vals_%d" % f, tag="vals_%d" % f, align_bytes=64)
            nc.sync.dma_start(whole[:], vals[f * P : (f + 1) * P, :])
            return whole

        raw0 = load_pieces(0, (0, 1024, 1536, 2048))
        prior_sb = keep.tile([P, U], F32, name="prior_sb")
        nc.sync.dma_start(prior_sb[:], prior)
        trust_sb = keep.tile([P, 1], F32, name="trust_sb", tag="trust")
        nc.sync.dma_start(trust_sb[:], trust)
        size_cols = keep.tile([P, PASSES, PACK], F32, name="size_cols")
        nc.sync.dma_start(size_cols[:], size.rearrange("o (h p c) -> p (o h) c", h=PASSES, c=PACK))
        raw1 = load_pieces(1, (512, 2048))
        raw2 = load_whole(2)
        raw1 = load_pieces(1, (0, 512)) + raw1
        raw3 = load_whole(3)

        ident = keep.tile([P, P], F32, name="ident")
        make_identity(nc, ident[:])
        minus_one = keep.tile([P, 1], F32, name="minus_one")
        nc.gpsimd.memset(minus_one[:], -1.0)

        q_grouped = keep.tile([P, Q, PACK], BF16, name="q_grouped", align_bytes=64)
        nc.scalar.copy(q_grouped[:], q_raw[:].rearrange("p j q -> p q j"))

        def pass_list(h):
            return slots[:, h * LIST_COLS : (h + 1) * LIST_COLS]

        k_scales = keep.tile([P, I], U8, name="k_scales", align_bytes=64)
        nc.vector.tensor_copy(k_scales[:], key_scales[:].indirect(slots[:]))

        def gather_keys(h):
            codes = keep.tile([P, PASS], U32, name="k_codes_%d" % h, tag="k_codes_%d" % h, align_bytes=64)
            nc.vector.tensor_copy(codes[:], key_words[:].bitcast(U32).indirect(pass_list(h)))
            return codes

        k_codes = [gather_keys(0)]
        q_codes = keep.tile([P, Q], U32, name="q_codes", align_bytes=64)
        q_scales = keep.tile([P, Q], U8, name="q_scales", align_bytes=64)
        nc.vector.quantize_mx(q_codes[:].bitcast(FP8X4), q_scales[:], q_grouped[:].rearrange("p q j -> p (q j)"))
        k_codes.append(gather_keys(1))

        scores = []
        for h in range(PASSES):
            bank = psum.tile([P, PASS], F32, name="scores_%d" % h, tag="bank_%d" % h)
            nc.tensor.matmul_mx(
                out=bank[:],
                lhsT=q_codes[:].bitcast(FP8X4),
                lhsT_scale=q_scales[:],
                rhs=k_codes[h][:].bitcast(FP8X4),
                rhs_scale=k_scales[:, h * PASS : (h + 1) * PASS],
                start=True,
                stop=True,
            )
            scores.append(bank)

        pool0 = keep.tile([P, T], BF16, name="pool0")
        for lo, hi, piece in raw0:
            nc.scalar.activation(pool0[:, lo:hi], piece[:], ACT.Copy)

        def gather_scalar(f, window, tag):
            picked = keep.tile([P, I], BF16, name="picked_%d" % f, tag=tag)
            nc.scalar.activation(picked[:], window[:].indirect(slots[:]), ACT.Copy)
            return picked

        def turn(rows, grouped, passes, copy):
            bank = turn_pool.tile([P, passes, 2, P], F32, name="turned", tag="turned")
            words = rows.bitcast(F32)
            for h in range(passes):
                for u in range(2):
                    lo = h * PASS // 2
                    nc.tensor.transpose(bank[:, h, u, :], words[:, lo + u : lo + PASS // 2 : 2], ident[:])
            copy(
                grouped.bitcast(F32).rearrange("p (h r u) -> p h r u", h=passes, u=2),
                bank[:].rearrange("p h u r -> p h r u"),
            )

        first = keep.tile([P, I], BF16, name="first", align_bytes=64)
        for h in range(PASSES):
            picked = keep.tile([P, PASS], BF16, name="picked_0_%d" % h)
            nc.scalar.activation(picked[:], pool0[:].indirect(pass_list(h)), ACT.Copy)
            turn(picked[:], first[:, h * PASS : (h + 1) * PASS], 1, nc.scalar.copy)

        size_rows = []
        for h in range(PASSES):
            bank = psum.tile([P, PACK, P], F32, name="size_%d" % h, tag="bank_%d" % (PASSES + h))
            for c in range(PACK):
                nc.tensor.transpose(bank[:, c, :], size_cols[:, h, c : c + 1].to_broadcast([P, P]), ident[:])
            size_rows.append(bank)

        trust16 = keep.tile([P, 1], F32, name="trust16")
        nc.gpsimd.tensor_scalar(trust16[:], trust_sb[:], float(PAGE), 0.0, ALU.mult, ALU.add)
        half_pages = G // PASSES

        def sum_pages(h, tag):
            sums = keep.tile([P, half_pages], F32, name="page_sums_%d" % h, tag=tag)
            nc.vector.tensor_reduce(sums[:], scores[h][:].rearrange("p (g j) -> p g j", j=PAGE), AX.X, ALU.add)
            return sums

        page_sums = [sum_pages(0, "page_sums_0")]
        prior_g = keep.tile([P, G], F32, name="prior_g")
        nc.vector.tensor_copy(prior_g[:], prior_sb[:].indirect(pages[:]))
        page_sums.append(sum_pages(1, "trust"))
        shift16 = []
        for h in range(PASSES):
            shift = keep.tile([P, half_pages], F32, name="shift16_%d" % h, tag="shift16_%d" % h, align_bytes=64)
            nc.vector.scalar_tensor_tensor(
                shift[:], prior_g[:, h * half_pages : (h + 1) * half_pages], trust16[:], page_sums[h][:], ALU.mult, ALU.subtract
            )
            shift16.append(shift)
        centred = keep.tile([P, I], F32, name="centred", tag="centred")
        for h in range(PASSES):
            nc.vector.scalar_tensor_tensor(
                centred[:, h * PASS : (h + 1) * PASS].rearrange("p (g j) -> p g j", j=PAGE),
                shift16[h][:].unsqueeze(2).to_broadcast([P, half_pages, PAGE]),
                1.0 / PAGE,
                scores[h][:].rearrange("p (g j) -> p g j", j=PAGE),
                ALU.mult,
                ALU.add,
            )
        half_max = []
        for h in range(PASSES):
            part = keep.tile([P, 1], F32, name="half_max_%d" % h)
            nc.vector.tensor_reduce(part[:], centred[:, h * PASS : (h + 1) * PASS], AX.X, ALU.max, negate=True)
            half_max.append(part)
        neg_max = keep.tile([P, 1], F32, name="neg_max", tag="neg_max", align_bytes=64)
        nc.gpsimd.tensor_scalar(neg_max[:], half_max[0][:], half_max[1][:], None, ALU.min)
        pool1 = keep.tile([P, T], BF16, name="pool1", tag="shift16_1", align_bytes=64)
        nc.vector.tensor_copy(pool1[:, raw1[1][0] : raw1[1][1]], raw1[1][2][:])

        probs = keep.tile([P, I], F32, name="probs")
        row_sum = keep.tile([P, 1], F32, name="row_sum", tag="inv_sum_dep")
        nc.scalar.activation(probs[:], centred[:], ACT.Exp, bias=neg_max[:], accum_out=row_sum[:])
        inv_sum = keep.tile([P, 1], F32, name="inv_sum")
        nc.gpsimd.tensor_tensor(inv_sum[:], row_sum[:], minus_one[:], ALU.pow)
        nc.scalar.activation(pool1[:, raw1[0][0] : raw1[0][1]], raw1[0][2][:], ACT.Copy)
        picked1 = gather_scalar(1, pool1, "picked_1")
        picked2 = keep.tile([P, I], BF16, name="picked_2", tag="picked_2")
        nc.vector.tensor_copy(picked2[:], raw2[:].indirect(slots[:]))

        w_rows = keep.tile([P, I], BF16, name="w_rows")
        for h in range(PASSES):
            nc.vector.scalar_tensor_tensor(
                w_rows[:, h * PASS : (h + 1) * PASS].rearrange("q (p c) -> q p c", c=PACK),
                probs[:, h * PASS : (h + 1) * PASS].rearrange("q (p c) -> q p c", c=PACK),
                inv_sum[:],
                size_rows[h][:].rearrange("q c p -> q p c"),
                ALU.mult,
                ALU.mult,
            )

        picked3 = []
        for h in range(PASSES):
            picked = keep.tile([P, PASS], BF16, name="picked_3_%d" % h)
            nc.vector.tensor_copy(picked[:], raw3[:].indirect(pass_list(h)))
            picked3.append(picked)

        grouped = keep.tile([P, 4 * I], BF16, name="grouped", tag="shift16_1", align_bytes=64)
        turn(picked2[:], grouped[:, I : 2 * I], PASSES, nc.scalar.copy)
        turn(w_rows[:], grouped[:, 0:I], PASSES, nc.scalar.copy)
        turn(picked1[:], grouped[:, 2 * I : 3 * I], PASSES, nc.scalar.copy)
        for h in range(PASSES):
            turn(picked3[h][:], grouped[:, 3 * I + h * PASS : 3 * I + (h + 1) * PASS], 1, nc.scalar.copy)

        width = PASSES * P
        codes = keep.tile([P, 5 * width], U32, name="codes", tag="vals_3", align_bytes=64)
        scales = keep.tile([P, 5 * width], U8, name="scales", align_bytes=64)

        def quantize(place, rows):
            cols = slice(place, place + rows.shape[1] // PACK)
            nc.vector.quantize_mx(codes[:, cols].bitcast(FP8X4), scales[:, cols], rows)

        quantize(4 * width, first[:])
        quantize(0, grouped[:, 0 : 2 * I])
        quantize(2 * width, grouped[:, 2 * I : 3 * I])
        for h in range(PASSES):
            quantize(3 * width + h * P, grouped[:, 3 * I + h * PASS : 3 * I + (h + 1) * PASS])

        for f, place in ((0, 4), (2, 1), (1, 2), (3, 3)):
            acc = psum.tile([P, P], F32, name="acc_%d" % f, tag="bank_%d" % f)
            for h in range(PASSES):
                w_cols = slice(h * P, (h + 1) * P)
                v_cols = slice(place * width + h * P, place * width + (h + 1) * P)
                nc.tensor.matmul_mx(
                    out=acc[:],
                    lhsT=codes[:, w_cols].bitcast(FP8X4),
                    lhsT_scale=scales[:, w_cols],
                    rhs=codes[:, v_cols].bitcast(FP8X4),
                    rhs_scale=scales[:, v_cols],
                    start=(h == 0),
                    stop=(h == PASSES - 1),
                )
            result = keep.tile([P, P], F32, name="result_%d" % f)
            if f == 3:
                nc.vector.tensor_copy(result[:], acc[:])
            else:
                nc.scalar.copy(result[:], acc[:])
            nc.sync.dma_start(out[:, f * P : (f + 1) * P], result[:])
